import numpy as np
import ml_dtypes

BF16 = ml_dtypes.bfloat16


def bf(x):
    return np.asarray(x, np.float32).astype(BF16)


def f32(x):
    return np.asarray(x, np.float32)


def f64(x):
    return np.asarray(x).astype(np.float64)


def striped(idx):
    return np.concatenate([l.reshape(-1, 16).T for l in idx])


def rows(idx, k):
    return np.tile(np.repeat(idx, 16, axis=0), (k // (16 * 8), 1))


def look(tab, idx):
    return np.take_along_axis(f64(tab), rows(idx, len(tab)), axis=1)


K, S, V, N = 256, 2048, 512, 512


def setup_inputs():
    return {"tab": f32(np.random.standard_normal((K, S))), "pos": f32(np.random.standard_normal((K, V))), "offs": striped(np.stack([np.random.permutation(S)[:N] for _ in range(8)]))}


def reference(tab, pos, offs):
    idx = np.stack([g.T.reshape(-1) for g in np.split(offs, 8)])
    x = np.maximum(look(tab, idx) - f64(pos) + 0.5, 0.0)
    return x

@@ -1,0 +1,30 @@
+import concourse.mybir as mybir
+
+F32 = mybir.dt.float32
+U16 = mybir.dt.uint16
+ALU = mybir.AluOpType
+
+P = 128
+MARGIN = 0.5
+
+
+def tile_lookup_hinge_sub_out_kernel(tc, tab, pos, offs, out):
+    nc = tc.nc
+    rows, window_columns = tab.shape
+    n = pos.shape[1]
+    with tc.tile_pool(name="held", bufs=1) as held:
+        lists = held.tile([P, n // 16], U16, name="lists")
+        nc.sync.dma_start(lists[:], offs)
+
+        for b in range(rows // P):
+            block = slice(b * P, (b + 1) * P)
+            window = held.tile([P, window_columns], F32, name=f"window{b}")
+            positives = held.tile([P, n], F32, name=f"positives{b}")
+            difference = held.tile([P, n], F32, name=f"difference{b}")
+            hinge = held.tile([P, n], F32, name=f"hinge{b}")
+
+            nc.sync.dma_start(window[:], tab[block, :])
+            nc.scalar.dma_start(positives[:], pos[block, :])
+            nc.vector.tensor_tensor(difference[:], window[:].indirect(lists[:]), positives[:], ALU.subtract)
+            nc.vector.tensor_scalar(hinge[:], difference[:], MARGIN, 0.0, ALU.add, ALU.max)
+            nc.scalar.dma_start(out[block, :], hinge[:])

@@ -27,4 +27,5 @@ def tile_lookup_hinge_sub_out_kernel(tc, tab, pos, offs, out):
             nc.scalar.dma_start(positives[:], pos[block, :])
             nc.vector.tensor_tensor(difference[:], window[:].indirect(lists[:]), positives[:], ALU.subtract)
             nc.vector.tensor_scalar(hinge[:], difference[:], MARGIN, 0.0, ALU.add, ALU.max)
-            nc.scalar.dma_start(out[block, :], hinge[:])
+            queue = nc.sync if block.stop == rows else nc.scalar
+            queue.dma_start(out[block, :], hinge[:])

@@ -12,20 +12,23 @@ def tile_lookup_hinge_sub_out_kernel(tc, tab, pos, offs, out):
     nc = tc.nc
     rows, window_columns = tab.shape
     n = pos.shape[1]
+    blocks = rows // P
+    tab_rows = tab.rearrange("(b q t) c -> t q b c", b=blocks, t=2)
+    out_rows = out.rearrange("(b q t) c -> t q b c", b=blocks, t=2)
+    pos_pairs = pos.rearrange("(b q t) c -> q b (t c)", b=blocks, t=2)
     with tc.tile_pool(name="held", bufs=1) as held:
         lists = held.tile([P, n // 16], U16, name="lists")
         nc.sync.dma_start(lists[:], offs)
+        positives = held.tile([P, 2 * n], F32, name="positives")
+        nc.scalar.dma_start(positives[:], pos_pairs)
 
-        for b in range(rows // P):
-            block = slice(b * P, (b + 1) * P)
-            window = held.tile([P, window_columns], F32, name=f"window{b}")
-            positives = held.tile([P, n], F32, name=f"positives{b}")
-            difference = held.tile([P, n], F32, name=f"difference{b}")
-            hinge = held.tile([P, n], F32, name=f"hinge{b}")
+        for t in range(2):
+            window = held.tile([P, window_columns], F32, name=f"window{t}")
+            difference = held.tile([P, n], F32, name=f"difference{t}")
+            hinge = held.tile([P, n], F32, name=f"hinge{t}")
 
-            nc.sync.dma_start(window[:], tab[block, :])
-            nc.scalar.dma_start(positives[:], pos[block, :])
-            nc.vector.tensor_tensor(difference[:], window[:].indirect(lists[:]), positives[:], ALU.subtract)
+            nc.sync.dma_start(window[:], tab_rows[t])
+            nc.vector.tensor_tensor(difference[:], window[:].indirect(lists[:]), positives[:, t * n:(t + 1) * n], ALU.subtract)
             nc.vector.tensor_scalar(hinge[:], difference[:], MARGIN, 0.0, ALU.add, ALU.max)
-            queue = nc.sync if block.stop == rows else nc.scalar
-            queue.dma_start(out[block, :], hinge[:])
+            queue = nc.sync if t == 1 else nc.scalar
+            queue.dma_start(out_rows[t], hinge[:])

@@ -18,7 +18,6 @@ def tile_lookup_hinge_sub_out_kernel(tc, tab, pos, offs, out):
     pos_pairs = pos.rearrange("(b q t) c -> q b (t c)", b=blocks, t=2)
     with tc.tile_pool(name="held", bufs=1) as held:
         lists = held.tile([P, n // 16], U16, name="lists")
-        nc.sync.dma_start(lists[:], offs)
         positives = held.tile([P, 2 * n], F32, name="positives")
         nc.scalar.dma_start(positives[:], pos_pairs)
 
@@ -28,6 +27,8 @@ def tile_lookup_hinge_sub_out_kernel(tc, tab, pos, offs, out):
             hinge = held.tile([P, n], F32, name=f"hinge{t}")
 
             nc.sync.dma_start(window[:], tab_rows[t])
+            if t == 0:
+                nc.sync.dma_start(lists[:], offs)
             nc.vector.tensor_tensor(difference[:], window[:].indirect(lists[:]), positives[:, t * n:(t + 1) * n], ALU.subtract)
             nc.vector.tensor_scalar(hinge[:], difference[:], MARGIN, 0.0, ALU.add, ALU.max)
             queue = nc.sync if t == 1 else nc.scalar

@@ -5,6 +5,7 @@ U16 = mybir.dt.uint16
 ALU = mybir.AluOpType
 
 P = 128
+BURST = 256
 MARGIN = 0.5
 
 
@@ -18,13 +19,13 @@ def tile_lookup_hinge_sub_out_kernel(tc, tab, pos, offs, out):
     pos_pairs = pos.rearrange("(b q t) c -> q b (t c)", b=blocks, t=2)
     with tc.tile_pool(name="held", bufs=1) as held:
         lists = held.tile([P, n // 16], U16, name="lists")
-        positives = held.tile([P, 2 * n], F32, name="positives")
+        positives = held.tile([P, 2 * n], F32, name="positives", align_bytes=BURST)
         nc.scalar.dma_start(positives[:], pos_pairs)
 
         for t in range(2):
-            window = held.tile([P, window_columns], F32, name=f"window{t}")
+            window = held.tile([P, window_columns], F32, name=f"window{t}", align_bytes=BURST)
             difference = held.tile([P, n], F32, name=f"difference{t}")
-            hinge = held.tile([P, n], F32, name=f"hinge{t}")
+            hinge = held.tile([P, n], F32, name=f"hinge{t}", align_bytes=BURST)
 
             nc.sync.dma_start(window[:], tab_rows[t])
             if t == 0:

@@ -31,6 +31,11 @@ def tile_lookup_hinge_sub_out_kernel(tc, tab, pos, offs, out):
             if t == 0:
                 nc.sync.dma_start(lists[:], offs)
             nc.vector.tensor_tensor(difference[:], window[:].indirect(lists[:]), positives[:, t * n:(t + 1) * n], ALU.subtract)
-            nc.vector.tensor_scalar(hinge[:], difference[:], MARGIN, 0.0, ALU.add, ALU.max)
-            queue = nc.sync if t == 1 else nc.scalar
-            queue.dma_start(out_rows[t], hinge[:])
+            if t == 0:
+                nc.vector.tensor_scalar(hinge[:], difference[:], MARGIN, 0.0, ALU.add, ALU.max)
+                nc.scalar.dma_start(out_rows[t], hinge[:])
+            else:
+                for half, queue in enumerate((nc.scalar, nc.sync)):
+                    columns = slice(half * n // 2, (half + 1) * n // 2)
+                    nc.vector.tensor_scalar(hinge[:, columns], difference[:, columns], MARGIN, 0.0, ALU.add, ALU.max)
+                    queue.dma_start(out_rows[t][:, :, columns], hinge[:, columns])

@@ -31,11 +31,8 @@ def tile_lookup_hinge_sub_out_kernel(tc, tab, pos, offs, out):
             if t == 0:
                 nc.sync.dma_start(lists[:], offs)
             nc.vector.tensor_tensor(difference[:], window[:].indirect(lists[:]), positives[:, t * n:(t + 1) * n], ALU.subtract)
-            if t == 0:
-                nc.vector.tensor_scalar(hinge[:], difference[:], MARGIN, 0.0, ALU.add, ALU.max)
-                nc.scalar.dma_start(out_rows[t], hinge[:])
-            else:
-                for half, queue in enumerate((nc.scalar, nc.sync)):
-                    columns = slice(half * n // 2, (half + 1) * n // 2)
-                    nc.vector.tensor_scalar(hinge[:, columns], difference[:, columns], MARGIN, 0.0, ALU.add, ALU.max)
-                    queue.dma_start(out_rows[t][:, :, columns], hinge[:, columns])
+            for half in range(2):
+                columns = slice(half * n // 2, (half + 1) * n // 2)
+                nc.vector.tensor_scalar(hinge[:, columns], difference[:, columns], MARGIN, 0.0, ALU.add, ALU.max)
+                queue = nc.sync if (t, half) == (1, 1) else nc.scalar
+                queue.dma_start(out_rows[t][:, :, columns], hinge[:, columns])

@@ -6,6 +6,7 @@ ALU = mybir.AluOpType
 
 P = 128
 BURST = 256
+QUARTER = 65536
 MARGIN = 0.5
 
 
@@ -17,15 +18,20 @@ def tile_lookup_hinge_sub_out_kernel(tc, tab, pos, offs, out):
     tab_rows = tab.rearrange("(b q t) c -> t q b c", b=blocks, t=2)
     out_rows = out.rearrange("(b q t) c -> t q b c", b=blocks, t=2)
     pos_pairs = pos.rearrange("(b q t) c -> q b (t c)", b=blocks, t=2)
-    with tc.tile_pool(name="held", bufs=1) as held:
+    with tc.tile_pool(name="held", bufs=1) as held, tc.tile_pool(name="placed", bufs=1) as placed:
         lists = held.tile([P, n // 16], U16, name="lists")
         positives = held.tile([P, 2 * n], F32, name="positives", align_bytes=BURST)
         nc.scalar.dma_start(positives[:], pos_pairs)
 
         for t in range(2):
-            window = held.tile([P, window_columns], F32, name=f"window{t}", align_bytes=BURST)
-            difference = held.tile([P, n], F32, name=f"difference{t}")
-            hinge = held.tile([P, n], F32, name=f"hinge{t}", align_bytes=BURST)
+            if t == 0:
+                window = held.tile([P, window_columns], F32, name="window0", align_bytes=BURST)
+                difference = held.tile([P, n], F32, name="difference0")
+                hinge = held.tile([P, n], F32, name="hinge0", align_bytes=BURST)
+            else:
+                window = placed.tile([P, window_columns], F32, name="window1", offset=QUARTER - window_columns * 4 // 2)
+                difference = placed.tile([P, n], F32, name="difference1", offset=2 * QUARTER)
+                hinge = placed.tile([P, n], F32, name="hinge1", offset=0, align_bytes=QUARTER)
 
             nc.sync.dma_start(window[:], tab_rows[t])
             if t == 0:

@@ -6,7 +6,6 @@ ALU = mybir.AluOpType
 
 P = 128
 BURST = 256
-QUARTER = 65536
 MARGIN = 0.5
 
 
@@ -15,30 +14,23 @@ def tile_lookup_hinge_sub_out_kernel(tc, tab, pos, offs, out):
     rows, window_columns = tab.shape
     n = pos.shape[1]
     blocks = rows // P
-    tab_rows = tab.rearrange("(b q t) c -> t q b c", b=blocks, t=2)
-    out_rows = out.rearrange("(b q t) c -> t q b c", b=blocks, t=2)
-    pos_pairs = pos.rearrange("(b q t) c -> q b (t c)", b=blocks, t=2)
-    with tc.tile_pool(name="held", bufs=1) as held, tc.tile_pool(name="placed", bufs=1) as placed:
+    with tc.tile_pool(name="held", bufs=1) as held:
         lists = held.tile([P, n // 16], U16, name="lists")
-        positives = held.tile([P, 2 * n], F32, name="positives", align_bytes=BURST)
-        nc.scalar.dma_start(positives[:], pos_pairs)
+        positives = held.tile([P, blocks, n], F32, name="positives", align_bytes=BURST)
+        nc.scalar.dma_start(positives[:], pos.rearrange("(b p) c -> p b c", b=blocks))
 
-        for t in range(2):
-            if t == 0:
-                window = held.tile([P, window_columns], F32, name="window0", align_bytes=BURST)
-                difference = held.tile([P, n], F32, name="difference0")
-                hinge = held.tile([P, n], F32, name="hinge0", align_bytes=BURST)
-            else:
-                window = placed.tile([P, window_columns], F32, name="window1", offset=QUARTER - window_columns * 4 // 2)
-                difference = placed.tile([P, n], F32, name="difference1", offset=2 * QUARTER)
-                hinge = placed.tile([P, n], F32, name="hinge1", offset=0, align_bytes=QUARTER)
+        for b in range(blocks):
+            block_rows = slice(b * P, (b + 1) * P)
+            window = held.tile([P, window_columns], F32, name=f"window{b}", align_bytes=BURST)
+            difference = held.tile([P, n], F32, name=f"difference{b}")
+            hinge = held.tile([P, n], F32, name=f"hinge{b}", align_bytes=BURST)
 
-            nc.sync.dma_start(window[:], tab_rows[t])
-            if t == 0:
+            nc.sync.dma_start(window[:], tab[block_rows, :])
+            if b == 0:
                 nc.sync.dma_start(lists[:], offs)
-            nc.vector.tensor_tensor(difference[:], window[:].indirect(lists[:]), positives[:, t * n:(t + 1) * n], ALU.subtract)
+            nc.vector.tensor_tensor(difference[:], window[:].indirect(lists[:]), positives[:, b, :], ALU.subtract)
             for half in range(2):
                 columns = slice(half * n // 2, (half + 1) * n // 2)
                 nc.vector.tensor_scalar(hinge[:, columns], difference[:, columns], MARGIN, 0.0, ALU.add, ALU.max)
-                queue = nc.sync if (t, half) == (1, 1) else nc.scalar
-                queue.dma_start(out_rows[t][:, :, columns], hinge[:, columns])
+                queue = nc.sync if (b, half) == (blocks - 1, 1) else nc.scalar
+                queue.dma_start(out[block_rows, columns], hinge[:, columns])

@@ -29,8 +29,10 @@ def tile_lookup_hinge_sub_out_kernel(tc, tab, pos, offs, out):
             if b == 0:
                 nc.sync.dma_start(lists[:], offs)
             nc.vector.tensor_tensor(difference[:], window[:].indirect(lists[:]), positives[:, b, :], ALU.subtract)
-            for half in range(2):
-                columns = slice(half * n // 2, (half + 1) * n // 2)
+            if b < blocks - 1:
+                pieces = [(slice(0, n), nc.sync)]
+            else:
+                pieces = [(slice(0, n // 4), nc.sync), (slice(n // 4, n // 2), nc.scalar), (slice(n // 2, n), nc.sync)]
+            for columns, queue in pieces:
                 nc.vector.tensor_scalar(hinge[:, columns], difference[:, columns], MARGIN, 0.0, ALU.add, ALU.max)
-                queue = nc.sync if (b, half) == (blocks - 1, 1) else nc.scalar
                 queue.dma_start(out[block_rows, columns], hinge[:, columns])

@@ -17,7 +17,6 @@ def tile_lookup_hinge_sub_out_kernel(tc, tab, pos, offs, out):
     with tc.tile_pool(name="held", bufs=1) as held:
         lists = held.tile([P, n // 16], U16, name="lists")
         positives = held.tile([P, blocks, n], F32, name="positives", align_bytes=BURST)
-        nc.scalar.dma_start(positives[:], pos.rearrange("(b p) c -> p b c", b=blocks))
 
         for b in range(blocks):
             block_rows = slice(b * P, (b + 1) * P)
@@ -28,9 +27,10 @@ def tile_lookup_hinge_sub_out_kernel(tc, tab, pos, offs, out):
             nc.sync.dma_start(window[:], tab[block_rows, :])
             if b == 0:
                 nc.sync.dma_start(lists[:], offs)
+                nc.sync.dma_start(positives[:], pos.rearrange("(b p) c -> p b c", b=blocks))
             nc.vector.tensor_tensor(difference[:], window[:].indirect(lists[:]), positives[:, b, :], ALU.subtract)
             if b < blocks - 1:
-                pieces = [(slice(0, n), nc.sync)]
+                pieces = [(slice(0, n), nc.scalar)]
             else:
                 pieces = [(slice(0, n // 4), nc.sync), (slice(n // 4, n // 2), nc.scalar), (slice(n // 2, n), nc.sync)]
             for columns, queue in pieces:

import concourse.mybir as mybir

F32 = mybir.dt.float32
U16 = mybir.dt.uint16
ALU = mybir.AluOpType

P = 128
BURST = 256
MARGIN = 0.5


def tile_lookup_hinge_sub_out_kernel(tc, tab, pos, offs, out):
    nc = tc.nc
    rows, window_columns = tab.shape
    n = pos.shape[1]
    blocks = rows // P
    with tc.tile_pool(name="held", bufs=1) as held:
        lists = held.tile([P, n // 16], U16, name="lists")
        positives = held.tile([P, blocks, n], F32, name="positives", align_bytes=BURST)

        for b in range(blocks):
            block_rows = slice(b * P, (b + 1) * P)
            window = held.tile([P, window_columns], F32, name=f"window{b}", align_bytes=BURST)
            difference = held.tile([P, n], F32, name=f"difference{b}")
            hinge = held.tile([P, n], F32, name=f"hinge{b}", align_bytes=BURST)

            nc.sync.dma_start(window[:], tab[block_rows, :])
            if b == 0:
                nc.sync.dma_start(lists[:], offs)
                nc.sync.dma_start(positives[:], pos.rearrange("(b p) c -> p b c", b=blocks))
            nc.vector.tensor_tensor(difference[:], window[:].indirect(lists[:]), positives[:, b, :], ALU.subtract)
            if b < blocks - 1:
                pieces = [(slice(0, n), nc.scalar)]
            else:
                pieces = [(slice(0, n // 4), nc.sync), (slice(n // 4, n // 2), nc.scalar), (slice(n // 2, n), nc.sync)]
            for columns, queue in pieces:
                nc.vector.tensor_scalar(hinge[:, columns], difference[:, columns], MARGIN, 0.0, ALU.add, ALU.max)
                queue.dma_start(out[block_rows, columns], hinge[:, columns])
